import numpy as np
import ml_dtypes

BF16 = ml_dtypes.bfloat16


def bf(x):
    return np.asarray(x, np.float32).astype(BF16)


def f32(x):
    return np.asarray(x, np.float32)


def f64(x):
    return np.asarray(x).astype(np.float64)


def striped(idx):
    return np.tile(idx.reshape(-1, 16).T, (8, 1))


S, K, M, N, V, D = 256, 256, 128, 64, 1, 256


def setup_inputs():
    return {"base": bf(np.random.standard_normal((M, S))), "x": bf(np.random.standard_normal((K, N))), "w": bf(1.5 * np.random.standard_normal((K, M)) / np.sqrt(K)), "s": f32(0.5 + np.random.random_sample((M, 1))), "offs": striped(np.random.permutation(S)[:N])}


def reference(base, x, w, s, offs):
    idx = offs[:16].T.reshape(-1)
    z = f64(base).copy()
    z[:, idx] += f64(w).T @ f64(x)
    z = z * f64(s)
    u = z.reshape(M, V, D)
    u = u - u.max(axis=2, keepdims=True)
    u = u - np.log(np.exp(u).sum(axis=2, keepdims=True))
    return u.reshape(M, S)

@@ -1,0 +1,63 @@
+import concourse.mybir as mybir
+from concourse.masks import make_identity
+
+BF16, F32, U16 = mybir.dt.bfloat16, mybir.dt.float32, mybir.dt.uint16
+ALU = mybir.AluOpType
+ACT = mybir.ActivationFunctionType
+P = 128
+
+FLOPS = 2 * 256 * 128 * 64
+
+
+def tile_rows_rescore_kernel(tc, base, x, w, s, offs, out):
+    nc = tc.nc
+    states, words = base.shape
+    features, entries = x.shape
+    blocks = features // P
+
+    with (
+        tc.tile_pool(name="held", bufs=1) as held,
+        tc.psum_pool(name="psum", bufs=1) as psum,
+    ):
+        base_tile = held.tile([P, words], BF16)
+        nc.sync.dma_start(base_tile[:], base)
+        offsets = held.tile([P, entries // 16], U16)
+        nc.sync.dma_start(offsets[:], offs)
+        x_tile = held.tile([P, blocks * entries], BF16)
+        nc.sync.dma_start(x_tile[:], x.rearrange("(p a) n -> p (a n)", a=blocks))
+        w_tile = held.tile([P, blocks * states], BF16)
+        nc.sync.dma_start(w_tile[:], w.rearrange("(p a) m -> p (a m)", a=blocks))
+        s_tile = held.tile([P, 1], F32)
+        nc.sync.dma_start(s_tile[:], s)
+
+        identity = held.tile([P, P], BF16)
+        make_identity(nc, identity[:])
+        neg_s = held.tile([P, 1], F32)
+        nc.vector.tensor_scalar_mul(neg_s[:], s_tile[:], -1.0)
+
+        window = psum.tile([P, words], F32)
+        nc.tensor.matmul(window[:], identity[:], base_tile[:], start=True, stop=False)
+        for a in range(blocks):
+            nc.tensor.matmul(
+                window[:].indirect(offsets[:]),
+                w_tile[:, a * states : (a + 1) * states],
+                x_tile[:, a * entries : (a + 1) * entries],
+                start=False,
+                stop=a == blocks - 1,
+            )
+
+        neg_t = held.tile([P, words], F32)
+        neg_max = held.tile([P, 1], F32)
+        nc.vector.tensor_scalar(neg_t[:], window[:], neg_s[:], None, ALU.mult, ALU.min, accum_out=neg_max[:])
+
+        exps = held.tile([P, words], F32)
+        exp_sum = held.tile([P, 1], F32)
+        nc.scalar.activation(exps[:], neg_t[:], ACT.Exp, bias=neg_max[:], scale=-1.0, accum_out=exp_sum[:])
+        log_sum = held.tile([P, 1], F32)
+        nc.scalar.activation(log_sum[:], exp_sum[:], ACT.Ln)
+
+        shifted = held.tile([P, words], F32)
+        nc.vector.tensor_scalar(shifted[:], neg_t[:], -1.0, neg_max[:], ALU.mult, ALU.add)
+        result = held.tile([P, words], F32)
+        nc.vector.tensor_scalar(result[:], shifted[:], log_sum[:], None, ALU.subtract)
+        nc.sync.dma_start(out, result[:])

@@ -1,3 +1,5 @@
+import math
+
 import concourse.mybir as mybir
 from concourse.masks import make_identity
 
@@ -6,7 +8,13 @@ ALU = mybir.AluOpType
 ACT = mybir.ActivationFunctionType
 P = 128
 
+I32 = mybir.dt.int32
 FLOPS = 2 * 256 * 128 * 64
+
+MANTISSA_BITS = 0x007FFFFF
+BITS_OF_ONE = 0x3F800000
+LN2 = math.log(2.0)
+LOG_POLYNOMIAL = (-0.01702961, 0.18370084, -0.8520796, 2.22694346, -3.6471204, 3.51208766, -1.40650067)
 
 
 def tile_rows_rescore_kernel(tc, base, x, w, s, offs, out):
@@ -35,6 +43,11 @@ def tile_rows_rescore_kernel(tc, base, x, w, s, offs, out):
         neg_s = held.tile([P, 1], F32)
         nc.vector.tensor_scalar_mul(neg_s[:], s_tile[:], -1.0)
 
+        powers = len(LOG_POLYNOMIAL) - 1
+        coefficients = held.tile([P, powers], F32)
+        for k in range(powers):
+            nc.vector.memset(coefficients[:, k : k + 1], LOG_POLYNOMIAL[k + 1])
+
         window = psum.tile([P, words], F32)
         nc.tensor.matmul(window[:], identity[:], base_tile[:], start=True, stop=False)
         for a in range(blocks):
@@ -53,11 +66,27 @@ def tile_rows_rescore_kernel(tc, base, x, w, s, offs, out):
         exps = held.tile([P, words], F32)
         exp_sum = held.tile([P, 1], F32)
         nc.scalar.activation(exps[:], neg_t[:], ACT.Exp, bias=neg_max[:], scale=-1.0, accum_out=exp_sum[:])
-        log_sum = held.tile([P, 1], F32)
-        nc.scalar.activation(log_sum[:], exp_sum[:], ACT.Ln)
 
         shifted = held.tile([P, words], F32)
         nc.vector.tensor_scalar(shifted[:], neg_t[:], -1.0, neg_max[:], ALU.mult, ALU.add)
+
+        sum_bits = exp_sum[:].bitcast(I32)
+        mantissa = held.tile([P, 1], I32)
+        nc.vector.tensor_scalar(mantissa[:], sum_bits, MANTISSA_BITS, BITS_OF_ONE, ALU.bitwise_and, ALU.bitwise_or)
+        line = held.tile([P, 1], F32)
+        nc.vector.tensor_scalar(line[:], sum_bits, -float(BITS_OF_ONE), LN2 / 2**23, ALU.add, ALU.mult)
+        curve = held.tile([P, powers], F32)
+        nc.vector.tensor_tensor_scan(
+            curve[:],
+            mantissa[:].bitcast(F32).to_broadcast([P, powers]),
+            coefficients[:],
+            LOG_POLYNOMIAL[0],
+            ALU.mult,
+            ALU.add,
+        )
+
         result = held.tile([P, words], F32)
-        nc.vector.tensor_scalar(result[:], shifted[:], log_sum[:], None, ALU.subtract)
+        nc.vector.tensor_scalar(
+            result[:], shifted[:], curve[:, powers - 1 : powers], line[:], ALU.subtract, ALU.subtract
+        )
         nc.sync.dma_start(out, result[:])

import math

import concourse.mybir as mybir
from concourse.masks import make_identity

BF16, F32, U16 = mybir.dt.bfloat16, mybir.dt.float32, mybir.dt.uint16
ALU = mybir.AluOpType
ACT = mybir.ActivationFunctionType
P = 128

I32 = mybir.dt.int32
FLOPS = 2 * 256 * 128 * 64

MANTISSA_BITS = 0x007FFFFF
BITS_OF_ONE = 0x3F800000
LN2 = math.log(2.0)
LOG_POLYNOMIAL = (-0.01702961, 0.18370084, -0.8520796, 2.22694346, -3.6471204, 3.51208766, -1.40650067)


def tile_rows_rescore_kernel(tc, base, x, w, s, offs, out):
    nc = tc.nc
    states, words = base.shape
    features, entries = x.shape
    blocks = features // P

    with (
        tc.tile_pool(name="held", bufs=1) as held,
        tc.psum_pool(name="psum", bufs=1) as psum,
    ):
        base_tile = held.tile([P, words], BF16)
        nc.sync.dma_start(base_tile[:], base)
        offsets = held.tile([P, entries // 16], U16)
        nc.sync.dma_start(offsets[:], offs)
        x_tile = held.tile([P, blocks * entries], BF16)
        nc.sync.dma_start(x_tile[:], x.rearrange("(p a) n -> p (a n)", a=blocks))
        w_tile = held.tile([P, blocks * states], BF16)
        nc.sync.dma_start(w_tile[:], w.rearrange("(p a) m -> p (a m)", a=blocks))
        s_tile = held.tile([P, 1], F32)
        nc.sync.dma_start(s_tile[:], s)

        identity = held.tile([P, P], BF16)
        make_identity(nc, identity[:])
        neg_s = held.tile([P, 1], F32)
        nc.vector.tensor_scalar_mul(neg_s[:], s_tile[:], -1.0)

        powers = len(LOG_POLYNOMIAL) - 1
        coefficients = held.tile([P, powers], F32)
        for k in range(powers):
            nc.vector.memset(coefficients[:, k : k + 1], LOG_POLYNOMIAL[k + 1])

        window = psum.tile([P, words], F32)
        nc.tensor.matmul(window[:], identity[:], base_tile[:], start=True, stop=False)
        for a in range(blocks):
            nc.tensor.matmul(
                window[:].indirect(offsets[:]),
                w_tile[:, a * states : (a + 1) * states],
                x_tile[:, a * entries : (a + 1) * entries],
                start=False,
                stop=a == blocks - 1,
            )

        neg_t = held.tile([P, words], F32)
        neg_max = held.tile([P, 1], F32)
        nc.vector.tensor_scalar(neg_t[:], window[:], neg_s[:], None, ALU.mult, ALU.min, accum_out=neg_max[:])

        exps = held.tile([P, words], F32)
        exp_sum = held.tile([P, 1], F32)
        nc.scalar.activation(exps[:], neg_t[:], ACT.Exp, bias=neg_max[:], scale=-1.0, accum_out=exp_sum[:])

        shifted = held.tile([P, words], F32)
        nc.vector.tensor_scalar(shifted[:], neg_t[:], -1.0, neg_max[:], ALU.mult, ALU.add)

        sum_bits = exp_sum[:].bitcast(I32)
        mantissa = held.tile([P, 1], I32)
        nc.vector.tensor_scalar(mantissa[:], sum_bits, MANTISSA_BITS, BITS_OF_ONE, ALU.bitwise_and, ALU.bitwise_or)
        line = held.tile([P, 1], F32)
        nc.vector.tensor_scalar(line[:], sum_bits, -float(BITS_OF_ONE), LN2 / 2**23, ALU.add, ALU.mult)
        curve = held.tile([P, powers], F32)
        nc.vector.tensor_tensor_scan(
            curve[:],
            mantissa[:].bitcast(F32).to_broadcast([P, powers]),
            coefficients[:],
            LOG_POLYNOMIAL[0],
            ALU.mult,
            ALU.add,
        )

        result = held.tile([P, words], F32)
        nc.vector.tensor_scalar(
            result[:], shifted[:], curve[:, powers - 1 : powers], line[:], ALU.subtract, ALU.subtract
        )
        nc.sync.dma_start(out, result[:])
